import numpy as np
import ml_dtypes


def mxq(x, axis, fmt="e4m3"):
    dtype, down = {"e4m3": (ml_dtypes.float8_e4m3fn, 7), "e5m2": (ml_dtypes.float8_e5m2, 14)}[fmt]
    v = np.moveaxis(np.asarray(x, np.float32).astype(ml_dtypes.bfloat16).astype(np.float64), axis, -1)
    blocks = v.reshape(v.shape[:-1] + (-1, 32))
    amax = np.abs(blocks).max(-1, keepdims=True)
    byte = np.maximum(np.where(amax > 0, np.frexp(amax)[1] - 1 + 127, 0) - down, 1)
    scale = np.exp2(byte - 127.0)
    codes = (blocks / scale).astype(np.float32).astype(dtype).astype(np.float64)
    return np.moveaxis((codes * scale).reshape(v.shape), -1, axis)


WIDE = False


def mx_kscale(k):
    if not WIDE:
        return np.ones(k)
    levels = np.array([10, -10, 5, -5, 0])
    if k % 512:
        return np.exp2(np.random.permutation(np.resize(levels, k // 32))).repeat(32)
    a = np.empty((k // 512, 16))
    for p in range(k // 512):
        a[p, :8] = np.random.permutation(np.resize(levels, 8))
        for g in range(8):
            far = levels[np.abs(levels - a[p, g]) >= 10]
            a[p, g + 8] = far[np.random.randint(len(far))]
    return np.exp2(a.ravel()).repeat(32)


def f64(x):
    return np.asarray(x).astype(np.float64)


def striped(idx):
    return np.tile(idx.reshape(-1, 16).T, (8, 1)).astype(np.uint16)


def unstriped(offs):
    return offs[:16].T.reshape(-1).astype(np.int64)


E2M1 = np.array([0.0, 0.5, 1.0, 1.5, 2.0, 3.0, 4.0, 6.0, -0.0, -0.5, -1.0, -1.5, -2.0, -3.0, -4.0, -6.0])


def pack_weight(w, fmt):
    k, n = w.shape
    w = f64(np.asarray(w, np.float32).astype(ml_dtypes.bfloat16)).reshape(k // 32, 32, n)
    amax = np.abs(w).max(1)
    if fmt == "e4m3":
        byte = np.frexp(amax)[1] - 1 + 127 - 7
    else:
        mant, ex = np.frexp(amax / 6.0)
        byte = np.where(mant > 0.5, ex, ex - 1) + 127
    byte = np.clip(np.where(amax > 0, byte, 1), 1, 254)
    scaled = (w * np.exp2(127.0 - byte)[:, None, :]).reshape(k, n).astype(np.float32)
    by_word = np.ascontiguousarray(scaled.reshape(k // 512, 128, 4, n).transpose(0, 1, 3, 2))
    if fmt == "e4m3":
        words = by_word.astype(ml_dtypes.float8_e4m3fn).view(np.uint8)
    else:
        c = by_word.astype(ml_dtypes.float4_e2m1fn).view(np.uint8) & 0xF
        words = (c[..., 0::2] | (c[..., 1::2] << 4)).reshape(k // 512, 128, 2 * n)
    return np.ascontiguousarray(words), np.ascontiguousarray(byte.astype(np.uint8).reshape(k // 512, 16, n))


def unpack_weight(words, scales, fmt):
    g, _, n = scales.shape
    words = np.ascontiguousarray(words).reshape(g, 128, n, -1)
    if fmt == "e4m3":
        vals = words.view(ml_dtypes.float8_e4m3fn).astype(np.float64)
    else:
        nib = np.empty((g, 128, n, 4), np.uint8)
        nib[..., 0::2] = words & 0xF
        nib[..., 1::2] = words >> 4
        vals = E2M1[nib]
    vals = vals * np.repeat(np.exp2(scales.astype(np.float64) - 127.0), 8, axis=1)[..., None]
    return vals.transpose(0, 1, 3, 2).reshape(g * 512, n)


def pack_table(v):
    words, scales = pack_weight(v, "e4m3")
    return np.concatenate([words.reshape(words.shape[0], -1), scales.reshape(scales.shape[0], -1)], axis=1)


def unpack_table(tab):
    g, t = tab.shape[0], tab.shape[1] // 528
    return unpack_weight(tab[:, :512 * t].reshape(g, 128, t, 4), tab[:, 512 * t:].reshape(g, 16, t), "e4m3")


K, M, T, S = 2048, 1024, 2048, 1024


def setup_inputs():
    n = np.random.standard_normal
    s = mx_kscale(K)[:, None]
    u = mx_kscale(512)[:, None]
    p_w4 = pack_weight(n((K, M)) / np.sqrt(K) / s, "e2m1")
    return {
        "tab": pack_table(n((K, T)) * s),
        "w4_words": p_w4[0],
        "w4_scales": p_w4[1],
        "down": (n((K, 512)) / np.sqrt(K) / s * u.T).astype(np.float32),
        "up": (0.5 * n((512, M)) / np.sqrt(512) / u).astype(np.float32),
        "b": (0.3 * n(1024)).astype(np.float32),
        "wgo": np.tile(np.random.uniform(0.5, 2.0, S), (128, 1)).astype(np.float32),
        "offs": striped(np.random.permutation(T)[:S]),
        "offs2": striped(np.random.permutation(T)[:S]),
    }


def reference(tab, w4_words, w4_scales, down, up, b, wgo, offs, offs2):
    tab_ = unpack_table(tab)[:, unstriped(offs)]
    w4_ = unpack_weight(w4_words, w4_scales, "e2m1")
    down_ = mxq(f64(down), 0, "e4m3")
    up_ = mxq(f64(up), 0, "e4m3")
    h_ = mxq(down_.T @ tab_, 0, "e4m3")
    y = w4_.T @ tab_ + up_.T @ h_
    out = np.zeros((M, T))
    out[:, unstriped(offs2)] = f64(wgo)[0] * (y + f64(b)[:, None])
    return out

from contextlib import ExitStack

import concourse.mybir as mybir
from concourse.masks import make_identity

K, M, T, S, R = 2048, 1024, 2048, 1024, 512
FLOPS = 2 * S * (K * M + K * R + R * M)

F32 = mybir.dt.float32
BF16 = mybir.dt.bfloat16
I32 = mybir.dt.int32
U32 = mybir.dt.uint32
U16 = mybir.dt.uint16
U8 = mybir.dt.uint8
FP8X4 = mybir.dt.float8_e4m3fn_x4
FP4X4 = mybir.dt.float4_e2m1fn_x4
IDENTITY = mybir.ActivationFunctionType.Identity
MULT = mybir.AluOpType.mult

P = 128
PACK = 4
K_PASS = P * PACK
PASSES = K // K_PASS
N_TILES = M // P
CHUNK = 128
CHUNKS = S // CHUNK
BANK = 512
EARLY = 256
WINDOWS = 3
PER_COL = 16
SHIFT_ROWS = 112


def tile_list_tabscat_l_bias_kernel(
    tc, tab, w4_words, w4_scales, down, up, b, wgo, offs, offs2, out
):
    nc = tc.nc
    with ExitStack() as ctx:
        keep = ctx.enter_context(tc.tile_pool(name="keep", bufs=1))
        ring = ctx.enter_context(tc.tile_pool(name="ring", bufs=3))
        psum = ctx.enter_context(tc.psum_pool(name="psum", bufs=1))

        def held(name, shape, dtype):
            return keep.tile(shape, dtype, name=name, align_bytes=64)

        def bank(i, shape):
            return psum.tile(shape, F32, name="bank%d" % i)

        pick = keep.tile([P, S // PER_COL], U16, name="pick")
        place = keep.tile([P, S // PER_COL], U16, name="place")
        tab_words = [held("tab_words%d" % a, [P, T], I32) for a in range(PASSES)]
        tab_scales = held("tab_scales", [P, T], U8)
        v_words = [held("v_words%d" % a, [P, S], U32) for a in range(PASSES)]
        v_packed = held("v_packed", [P, S], U8)
        v_planes = [v_packed] + [held("v_plane%d" % a, [P, S], U8) for a in range(1, PASSES)]
        down_raw = [held("down_raw%d" % a, [P, PACK, R], F32) for a in range(PASSES)]
        down_bf = [held("down_bf%d" % a, [P, PACK * R], BF16) for a in range(PASSES)]
        down_codes = [held("down_codes%d" % a, [P, R], U32) for a in range(PASSES)]
        down_scales = [held("down_scales%d" % a, [P, R], U8) for a in range(PASSES)]
        col_ranges = [(0, EARLY), (EARLY, M)]
        up_raw = [held("up_raw%d" % g, [P, PACK, c1 - c0], F32) for g, (c0, c1) in enumerate(col_ranges)]
        w4_codes = [held("w4_codes%d" % g, [P, PASSES, 2 * (c1 - c0)], U8) for g, (c0, c1) in enumerate(col_ranges)]
        w4_planes = [held("w4_planes%d" % g, [P, PASSES, c1 - c0], U8) for g, (c0, c1) in enumerate(col_ranges)]
        up_bf = held("up_bf", [P, PACK * M], BF16)
        up_codes = held("up_codes", [P, M], U32)
        up_scales = held("up_scales", [P, M], U8)
        h_bf = held("h_bf", [P, PACK * S], BF16)
        h_codes = held("h_codes", [P, S], U32)
        h_scales = held("h_scales", [P, S], U8)
        weight = held("weight", [P, S], F32)
        b_rows = held("b_rows", [P, P], F32)
        ident = held("ident", [P, P], F32)
        bias = held("bias", [P, N_TILES], F32)
        windows = [held("window%d" % w, [P, T], F32) for w in range(WINDOWS)]

        def load_tab_words(a):
            src = tab[a, 0 : K_PASS * T].rearrange("(p c) -> p c", p=P).bitcast(I32)
            nc.sync.dma_start(out=tab_words[a][:], in_=src)

        def load_tab_scales():
            rows = tab[:, K_PASS * T :].rearrange("a (q t) -> a q t", t=T).bitcast(I32)
            for quad in range(4):
                nc.sync.dma_start(
                    out=tab_scales[32 * quad : 32 * quad + 16, :].bitcast(I32),
                    in_=rows[:, 4 * quad : 4 * quad + 4, :],
                )

        def load_down(a):
            rows = down[a * K_PASS : (a + 1) * K_PASS, :]
            nc.sync.dma_start(out=down_raw[a][:], in_=rows.rearrange("(p j) r -> p j r", j=PACK))

        def load_up(g):
            c0, c1 = col_ranges[g]
            nc.sync.dma_start(out=up_raw[g][:], in_=up[:, c0:c1].rearrange("(p j) n -> p j n", j=PACK))

        def load_w4(g):
            c0, c1 = col_ranges[g]
            src = w4_words.rearrange("a p c -> p a c")[:, :, 2 * c0 : 2 * c1]
            nc.sync.dma_start(out=w4_codes[g][:].bitcast(I32), in_=src.bitcast(I32))
            rows = w4_scales.rearrange("a q n -> q a n")[:, :, c0:c1].bitcast(I32)
            for quad in range(4):
                nc.sync.dma_start(
                    out=w4_planes[g][32 * quad : 32 * quad + 4, :, :].bitcast(I32),
                    in_=rows[4 * quad : 4 * quad + 4, :, :],
                )

        def entries(offsets, j0, j1):
            return offsets[:, j0 // PER_COL : j1 // PER_COL]

        def gather_words(a, j0, j1):
            window = tab_words[a][:].bitcast(U32)
            nc.vector.tensor_copy(out=v_words[a][:, j0:j1], in_=window.indirect(entries(pick, j0, j1)))

        def round_down(a, m0, m1, copy):
            src = down_raw[a][:].rearrange("p j (m t) -> p m j t", t=PACK)
            dst = down_bf[a][:].rearrange("p (t m j) -> p m j t", t=PACK, j=PACK)
            copy(out=dst[:, m0:m1], in_=src[:, m0:m1])

        def quantize_down(a):
            nc.vector.quantize_mx(
                out=down_codes[a][:].bitcast(FP8X4), scales=down_scales[a][:], in_=down_bf[a][:]
            )

        def round_up(n0, n1, copy):
            g = 0 if n0 < EARLY else 1
            c0 = col_ranges[g][0]
            src = up_raw[g][:, :, n0 - c0 : n1 - c0].rearrange("p j (c i) -> p c j i", i=4)
            dst = up_bf[:, PACK * n0 : PACK * n1].rearrange("p (c i j) -> p c j i", i=4, j=PACK)
            copy(out=dst, in_=src)

        def quantize_up(n0, n1):
            nc.vector.quantize_mx(
                out=up_codes[:, n0:n1].bitcast(FP8X4),
                scales=up_scales[:, n0:n1],
                in_=up_bf[:, PACK * n0 : PACK * n1],
            )

        h_banks = {}

        def h_pass(a, c):
            if a == 0:
                h_banks[c] = bank(c, [P, PACK, CHUNK])
            cols = slice(c * CHUNK, (c + 1) * CHUNK)
            for t in range(PACK):
                slot = slice(t * P, (t + 1) * P)
                nc.tensor.matmul_mx(
                    out=h_banks[c][:, t, :],
                    lhsT=down_codes[a][:, slot].bitcast(FP8X4),
                    lhsT_scale=down_scales[a][:, slot],
                    rhs=v_words[a][:, cols].bitcast(FP8X4),
                    rhs_scale=v_packed[4 * a : P, cols],
                    start=(a == 0 and t == 0),
                    stop=(a == PASSES - 1 and t == PACK - 1),
                )

        def round_h(c):
            dst = h_bf[:, PACK * c * CHUNK : PACK * (c + 1) * CHUNK].rearrange("p (s t) -> p s t", t=PACK)
            nc.scalar.copy(out=dst, in_=h_banks[c][:].rearrange("p t s -> p s t"))

        def quantize_h(j0, j1):
            nc.vector.quantize_mx(
                out=h_codes[:, j0:j1].bitcast(FP8X4),
                scales=h_scales[:, j0:j1],
                in_=h_bf[:, PACK * j0 : PACK * j1],
            )

        banks_used = []

        def project(n, j0, j1):
            g = 0 if n * P < EARLY else 1
            c0 = n * P - col_ranges[g][0]
            y = ring.tile([P, S], F32, name="y")
            for s0 in range(j0, j1, BANK):
                s1 = min(j1, s0 + BANK)
                acc = bank(len(banks_used) % CHUNKS, [P, BANK])
                banks_used.append(n)
                width = BANK if s1 - s0 == BANK else CHUNK
                spans = list(range(s0, s1, width))
                for a in range(PASSES):
                    for s in spans:
                        nc.tensor.matmul_mx(
                            out=acc[:, s - s0 : s - s0 + width],
                            lhsT=w4_codes[g][:, a, 2 * c0 : 2 * (c0 + P)].bitcast(FP4X4),
                            lhsT_scale=w4_planes[g][:, a, c0 : c0 + P],
                            rhs=v_words[a][:, s : s + width].bitcast(FP8X4),
                            rhs_scale=v_planes[a][:, s : s + width],
                            start=(a == 0 and s == s0),
                            stop=False,
                        )
                for s in spans:
                    nc.tensor.matmul_mx(
                        out=acc[:, s - s0 : s - s0 + width],
                        lhsT=up_codes[:, n * P : (n + 1) * P].bitcast(FP8X4),
                        lhsT_scale=up_scales[:, n * P : (n + 1) * P],
                        rhs=h_codes[:, s : s + width].bitcast(FP8X4),
                        rhs_scale=h_scales[:, s : s + width],
                        start=False,
                        stop=(s == spans[-1]),
                    )
                nc.scalar.activation(
                    out=y[:, s0 - j0 : s1 - j0], in_=acc[:, 0 : s1 - s0], func=IDENTITY, bias=bias[:, n : n + 1]
                )
            window = windows[n % WINDOWS]
            nc.vector.tensor_tensor(
                out=window[:].indirect(entries(place, j0, j1)), in0=y[:, 0 : j1 - j0], in1=weight[:, j0:j1], op=MULT
            )
            if j1 == S:
                nc.sync.dma_start(out=out[n * P : (n + 1) * P, :], in_=window[:])

        nc.vector.memset(tab_scales[:].bitcast(I32), 0)
        nc.gpsimd.memset(b_rows[:], 0.0)
        make_identity(nc, ident[:])
        for a in range(1, PASSES):
            nc.vector.memset(v_planes[a][:].bitcast(I32), 0)
        for g in range(2):
            nc.vector.memset(w4_planes[g][:].bitcast(I32), 0)
        for w in range(WINDOWS):
            nc.vector.memset(windows[w][:], 0.0)

        nc.sync.dma_start(pick[:], offs)
        load_tab_words(0)
        load_tab_scales()
        load_down(0)
        load_tab_words(1)
        nc.sync.dma_start(out=b_rows[0:N_TILES, :], in_=b.rearrange("(n p) -> n p", p=P))
        nc.sync.dma_start(place[:], offs2)
        load_down(1)
        load_tab_words(2)
        load_down(2)
        load_down(3)
        load_tab_words(3)
        load_up(0)
        load_w4(0)
        nc.sync.dma_start(out=weight[:, 0:EARLY], in_=wgo[:, 0:EARLY])
        nc.sync.dma_start(out=weight[:, EARLY:S], in_=wgo[:, EARLY:S])
        load_up(1)
        load_w4(1)

        b_psum = bank(CHUNKS - 1, [P, P])
        nc.tensor.transpose(b_psum[:], b_rows[:], ident[:])
        nc.scalar.activation(out=bias[:], in_=b_psum[:, 0:N_TILES], func=IDENTITY)

        gather_words(0, 0, S)
        nc.vector.tensor_copy(out=v_packed[:], in_=tab_scales[:].indirect(pick[:]))
        for a in range(1, PASSES):
            nc.gpsimd.dma_start(
                out=v_planes[a][0:SHIFT_ROWS, :].bitcast(I32),
                in_=v_packed[4 * a : 4 * a + SHIFT_ROWS, :].bitcast(I32),
            )
        for a in range(PASSES - 1):
            if a > 0:
                gather_words(a, 0, S)
            round_down(a, 0, P, nc.scalar.copy)
            quantize_down(a)
            for c in range(CHUNKS):
                h_pass(a, c)
        last = PASSES - 1
        round_down(last, 0, 88, nc.vector.tensor_copy)
        round_down(last, 88, P, nc.scalar.copy)
        quantize_down(last)

        slices = [(0, 256), (256, 512), (512, 1024)]
        for j0, j1 in slices:
            gather_words(last, j0, j1)
            for c in range(j0 // CHUNK, j1 // CHUNK):
                h_pass(last, c)
                round_h(c)
            if j0 == 0:
                for n in range(EARLY // P):
                    round_up(n * P, (n + 1) * P, nc.vector.tensor_copy)
                    quantize_up(n * P, (n + 1) * P)
        for j0, j1 in slices:
            quantize_h(j0, j1)
            for n in range(EARLY // P):
                project(n, j0, j1)
        for n in range(EARLY // P, N_TILES):
            if n % 2 == 0:
                round_up(n * P, (n + 2) * P, nc.scalar.copy)
                quantize_up(n * P, (n + 2) * P)
            project(n, 0, S)
